import numpy as np
import ml_dtypes


def mxq(x, axis, fmt="e4m3"):
    dtype, down = {"e4m3": (ml_dtypes.float8_e4m3fn, 7), "e5m2": (ml_dtypes.float8_e5m2, 14)}[fmt]
    v = np.moveaxis(np.asarray(x, np.float32).astype(ml_dtypes.bfloat16).astype(np.float64), axis, -1)
    blocks = v.reshape(v.shape[:-1] + (-1, 32))
    amax = np.abs(blocks).max(-1, keepdims=True)
    byte = np.maximum(np.where(amax > 0, np.frexp(amax)[1] - 1 + 127, 0) - down, 1)
    scale = np.exp2(byte - 127.0)
    codes = (blocks / scale).astype(np.float32).astype(dtype).astype(np.float64)
    return np.moveaxis((codes * scale).reshape(v.shape), -1, axis)


WIDE = False


def mx_kscale(k):
    if not WIDE:
        return np.ones(k)
    levels = np.array([30, -30])
    if k % 512:
        return np.exp2(np.random.permutation(np.resize(levels, k // 32))).repeat(32)
    a = np.empty((k // 512, 16))
    for p in range(k // 512):
        a[p, :8] = np.random.permutation(np.resize(levels, 8))
        for g in range(8):
            far = levels[np.abs(levels - a[p, g]) >= 10]
            a[p, g + 8] = far[np.random.randint(len(far))]
    return np.exp2(a.ravel()).repeat(32)


def f64(x):
    return np.asarray(x).astype(np.float64)


def striped(idx):
    return np.tile(np.asarray(idx).reshape(-1, 16).T, (8, 1)).astype(np.uint16)


def unstriped(offs):
    return offs[:16].T.reshape(-1).astype(np.int64)


E2M1 = np.array([0.0, 0.5, 1.0, 1.5, 2.0, 3.0, 4.0, 6.0, -0.0, -0.5, -1.0, -1.5, -2.0, -3.0, -4.0, -6.0])


def pack_weight(w, fmt):
    k, n = w.shape
    w = f64(np.asarray(w, np.float32).astype(ml_dtypes.bfloat16)).reshape(k // 32, 32, n)
    amax = np.abs(w).max(1)
    if fmt in ("e4m3", "e5m2"):
        byte = np.frexp(amax)[1] - 1 + 127 - (7 if fmt == "e4m3" else 14)
    else:
        mant, ex = np.frexp(amax / 6.0)
        byte = np.where(mant > 0.5, ex, ex - 1) + 127
    byte = np.clip(np.where(amax > 0, byte, 1), 1, 254)
    scaled = (w * np.exp2(127.0 - byte)[:, None, :]).reshape(k, n).astype(np.float32)
    by_word = np.ascontiguousarray(scaled.reshape(k // 512, 128, 4, n).transpose(0, 1, 3, 2))
    if fmt in ("e4m3", "e5m2"):
        words = by_word.astype(ml_dtypes.float8_e4m3fn if fmt == "e4m3" else ml_dtypes.float8_e5m2).view(np.uint8)
    else:
        c = by_word.astype(ml_dtypes.float4_e2m1fn).view(np.uint8) & 0xF
        words = (c[..., 0::2] | (c[..., 1::2] << 4)).reshape(k // 512, 128, 2 * n)
    return np.ascontiguousarray(words), np.ascontiguousarray(byte.astype(np.uint8).reshape(k // 512, 16, n))


def unpack_weight(words, scales, fmt):
    g, _, n = scales.shape
    words = np.ascontiguousarray(words).reshape(g, 128, n, -1)
    if fmt in ("e4m3", "e5m2"):
        vals = words.view(ml_dtypes.float8_e4m3fn if fmt == "e4m3" else ml_dtypes.float8_e5m2).astype(np.float64)
    else:
        nib = np.empty((g, 128, n, 4), np.uint8)
        nib[..., 0::2] = words & 0xF
        nib[..., 1::2] = words >> 4
        vals = E2M1[nib]
    vals = vals * np.repeat(np.exp2(scales.astype(np.float64) - 127.0), 8, axis=1)[..., None]
    return vals.transpose(0, 1, 3, 2).reshape(g * 512, n)


K, T, J, R, V, N, Z, E = 512, 2048, 256, 512, 512, 256, 1024, 1024


def setup_inputs():
    n = np.random.standard_normal
    idx = np.random.permutation(T)[:J]
    idx2 = np.random.permutation(Z)[:J]
    idx3 = np.random.permutation(V)[:J]
    idx4 = np.random.permutation(V)[:J]
    idx5 = np.random.permutation(E)[:J]
    fk = mx_kscale(K)
    fr = mx_kscale(R)
    xtp = pack_weight(n((K, T)) / fk[:, None], "e2m1")
    wp = pack_weight(n((K, R)) * 1 / np.sqrt(K) * fk[:, None] * fr, "e5m2")
    xop = pack_weight(n((K, Z)) / fk[:, None], "e5m2")
    wbp = pack_weight(n((R, N)) * 1 / np.sqrt(R) / fr[:, None], "e4m3")
    return {
        "xt_words": xtp[0],
        "xt_scales": xtp[1],
        "w_words": wp[0],
        "w_scales": wp[1],
        "xo_words": xop[0],
        "xo_scales": xop[1],
        "tb": (n((R, V))).astype(np.float32),
        "wb_words": wbp[0],
        "wb_scales": wbp[1],
        "offs": striped(idx),
        "offs2": striped(idx2),
        "offs3": striped(idx3),
        "offs4": striped(idx4),
        "offs5": striped(idx5),
    }


def reference(xt_words, xt_scales, w_words, w_scales, xo_words, xo_scales, tb, wb_words, wb_scales, offs, offs2, offs3, offs4, offs5):
    idx = unstriped(offs)
    idx2 = unstriped(offs2)
    idx3 = unstriped(offs3)
    idx4 = unstriped(offs4)
    idx5 = unstriped(offs5)
    xtu = unpack_weight(xt_words, xt_scales, "e2m1")
    wu = unpack_weight(w_words, w_scales, "e5m2")
    xou = unpack_weight(xo_words, xo_scales, "e5m2")
    wbu = unpack_weight(wb_words, wb_scales, "e4m3")
    xtidxg = xtu[:, idx]
    a = wu.T @ xtidxg
    xoidx2g = xou[:, idx2]
    da = wu.T @ xoidx2g
    hid = a * f64(tb)[:, idx3]
    dh = da * f64(tb)[:, idx3] + a * f64(tb)[:, idx4]
    hidq = mxq(hid, 0, "e5m2")
    p = wbu.T @ hidq
    dhq = mxq(dh, 0, "e4m3")
    dp = wbu.T @ dhq
    m0 = np.maximum(p, dp)
    y = np.zeros((N, E))
    y[:, idx5] = m0
    return y

from contextlib import ExitStack

import concourse.mybir as mybir

K, T, J, R, V, N, Z, E = 512, 2048, 256, 512, 512, 256, 1024, 1024
FLOPS = 2 * (2 * K * R * J + 2 * R * N * J)

F32 = mybir.dt.float32
BF16 = mybir.dt.bfloat16
I32 = mybir.dt.int32
U32 = mybir.dt.uint32
U16 = mybir.dt.uint16
U8 = mybir.dt.uint8
E2M1 = mybir.dt.float4_e2m1fn_x4
E5M2 = mybir.dt.float8_e5m2_x4
E4M3 = mybir.dt.float8_e4m3fn_x4
ALU = mybir.AluOpType
COPY = mybir.ActivationFunctionType.Copy

P = 128
PACK = 4
H = 128
HALVES = J // H
NT = N // P


def tile_list_firstorder_notes_scattered_kernel(
    tc, xt_words, xt_scales, w_words, w_scales, xo_words, xo_scales, tb, wb_words, wb_scales,
    offs, offs2, offs3, offs4, offs5, out,
):
    nc = tc.nc
    with ExitStack() as ctx:
        sb = ctx.enter_context(tc.tile_pool(name="sb", bufs=1))
        ps = ctx.enter_context(tc.psum_pool(name="ps", bufs=1))

        def tile(name, shape, dtype):
            return sb.tile(shape, dtype, name=name, align_bytes=64)

        def load_scales(queue, plane, rows):
            for q in range(4):
                queue.dma_start(plane[32 * q : 32 * q + 4, :].bitcast(I32), rows[0, 4 * q : 4 * q + 4, :].bitcast(I32))

        def load_words(dst, words):
            nc.sync.dma_start(dst[:].bitcast(I32), words.bitcast(I32))

        l1 = tile("l1", [P, J // 16], U16)
        l2 = tile("l2", [P, J // 16], U16)
        l3 = tile("l3", [P, J // 16], U16)
        l4 = tile("l4", [P, J // 16], U16)
        l5 = tile("l5", [P, J // 16], U16)
        xt_w = tile("xt_w", [P, T], U16)
        xt_s = tile("xt_s", [P, T], U8)
        xo_w = tile("xo_w", [P, Z], U32)
        xo_s = tile("xo_s", [P, Z], U8)
        w_w = tile("w_w", [P, R], I32)
        w_s = tile("w_s", [P, R], U8)
        wb_w = tile("wb_w", [P, N], U32)
        wb_s = tile("wb_s", [P, N], U8)
        tbs = [tile(f"tb{u}", [P, 2 * V], F32) for u in range(2)]
        pages = [tile(f"page{n}", [P, E], F32) for n in range(NT)]

        for plane in (w_s, xo_s, xt_s, wb_s):
            nc.vector.memset(plane[:].bitcast(I32), 0)
        for page in pages:
            nc.vector.memset(page[:], 0.0)

        tb_rows = tb.rearrange("(p u t) v -> p u (t v)", u=2, t=2)
        nc.sync.dma_start(l3[:], offs3)
        nc.sync.dma_start(l1[:], offs)
        load_scales(nc.sync, w_s, w_scales)
        nc.sync.dma_start(tbs[0][:], tb_rows[:, 0, :])
        load_words(xt_w, xt_words[0])
        load_scales(nc.gpsimd, xo_s, xo_scales)
        load_scales(nc.sync, xt_s, xt_scales)
        load_words(w_w, w_words[0].rearrange("p n t -> p (n t)"))
        nc.sync.dma_start(l4[:], offs4)
        nc.sync.dma_start(tbs[1][:], tb_rows[:, 1, :])
        load_words(xo_w, xo_words[0].rearrange("p n t -> p (n t)"))
        nc.sync.dma_start(l2[:], offs2)
        load_words(wb_w, wb_words[0].rearrange("p n t -> p (n t)"))
        nc.sync.dma_start(l5[:], offs5)
        load_scales(nc.sync, wb_s, wb_scales)

        t3all = tile("t3all", [P, PACK, J], F32)
        t4all = tile("t4all", [P, PACK, J], F32)

        def look_up(dst, lst, t):
            window = tbs[t // 2][:, (t % 2) * V : (t % 2 + 1) * V]
            nc.scalar.activation(out=dst[:, t, :], in_=window.indirect(lst[:]), func=COPY)

        for dst, lst, t in ((t3all, l3, 0), (t3all, l3, 1), (t4all, l4, 0), (t4all, l4, 1),
                            (t3all, l3, 2), (t3all, l3, 3), (t4all, l4, 2), (t4all, l4, 3)):
            look_up(dst, lst, t)

        xt_gw = tile("xt_gw", [P, J], U16)
        xt_gs = tile("xt_gs", [P, J], U8)
        xo_gw = tile("xo_gw", [P, J], U32)
        xo_gs = tile("xo_gs", [P, J], U8)
        nc.vector.tensor_copy(xt_gw[:], xt_w[:].indirect(l1[:]))
        nc.vector.tensor_copy(xt_gs[:], xt_s[:].indirect(l1[:]))

        w_pw = tile("w_pw", [P, R], I32)
        w_ps = tile("w_ps", [P, R], U8)
        nc.vector.tensor_copy(w_pw[:].rearrange("p (t m) -> p m t", t=PACK), w_w[:].rearrange("p (m t) -> p m t", t=PACK))
        nc.vector.tensor_copy(w_ps[:].rearrange("p (t m) -> p m t", t=PACK), w_s[:].rearrange("p (m t) -> p m t", t=PACK))

        def first_stage(name, words, scales, fmt):
            banks = []
            for h in range(HALVES):
                bank = ps.tile([P, PACK, H], F32, name=f"{name}{h}")
                js = slice(h * H, (h + 1) * H)
                for t in range(PACK):
                    rs = slice(t * P, (t + 1) * P)
                    nc.tensor.matmul_mx(out=bank[:, t, :], lhsT=w_pw[:, rs].bitcast(E5M2), lhsT_scale=w_ps[:, rs],
                                        rhs=words[:, js].bitcast(fmt), rhs_scale=scales[:, js], start=True, stop=True)
                banks.append(bank)
            return banks

        a = first_stage("a", xt_gw, xt_gs, E2M1)

        v = [tile(f"v{h}", [P, PACK, H], F32) for h in range(HALVES)]
        u_ = [tile(f"u{h}", [P, PACK, H], F32) for h in range(HALVES)]

        def product(dst, banks, table, h, u):
            ts = slice(2 * u, 2 * u + 2)
            nc.vector.tensor_tensor(dst[h][:, ts, :], banks[h][:, ts, :], table[:, ts, h * H : (h + 1) * H], ALU.mult)

        for h in range(HALVES):
            product(v, a, t4all, h, 0)

        nc.vector.tensor_copy(xo_gw[:], xo_w[:].indirect(l2[:]))
        nc.vector.tensor_copy(xo_gs[:], xo_s[:].indirect(l2[:]))
        da = first_stage("da", xo_gw, xo_gs, E5M2)

        def walk(ap):
            return ap.rearrange("p t (c i) -> p c t i", i=4)

        def woven(ap):
            return ap.rearrange("p (c i t) -> p c t i", i=4, t=PACK)

        hid = tile("hid", [P, J * PACK], BF16)
        for h in range(HALVES):
            nc.vector.tensor_tensor(woven(hid[:, h * H * PACK : (h + 1) * H * PACK]), walk(a[h][:]),
                                    walk(t3all[:, :, h * H : (h + 1) * H]), ALU.mult)
        for h in range(HALVES):
            product(u_, da, t3all, h, 0)
        hid_w = tile("hid_w", [P, J], U32)
        hid_s = tile("hid_s", [P, J], U8)
        nc.vector.quantize_mx(out=hid_w[:].bitcast(E5M2), scales=hid_s[:], in_=hid[:])
        p_bank = ps.tile([P, NT, J], F32, name="p_bank")
        for n in range(NT):
            ns = slice(n * P, (n + 1) * P)
            nc.tensor.matmul_mx(out=p_bank[:, n, :], lhsT=wb_w[:, ns].bitcast(E4M3), lhsT_scale=wb_s[:, ns],
                                rhs=hid_w[:].bitcast(E5M2), rhs_scale=hid_s[:], start=True, stop=True)
        p_sb = tile("p_sb", [P, NT, J], F32)
        nc.scalar.copy(p_sb[:], p_bank[:])

        dh = [tile(f"dh{h}", [P, H * PACK], BF16) for h in range(HALVES)]
        dh_w = [tile(f"dh_w{h}", [P, H], U32) for h in range(HALVES)]
        dh_s = [tile(f"dh_s{h}", [P, H], U8) for h in range(HALVES)]
        m0 = [tile(f"m0_{h}", [P, NT, H], F32) for h in range(HALVES)]
        dp = [ps.tile([P, NT, H], F32, name=f"dp{h}") for h in range(HALVES)]

        def finish_products(h):
            product(u_, da, t3all, h, 1)
            product(v, a, t4all, h, 1)

        def add(h):
            nc.vector.tensor_tensor(woven(dh[h][:]), walk(u_[h][:]), walk(v[h][:]), ALU.add)

        def second(h):
            nc.vector.quantize_mx(out=dh_w[h][:].bitcast(E4M3), scales=dh_s[h][:], in_=dh[h][:])
            for n in range(NT):
                ns = slice(n * P, (n + 1) * P)
                nc.tensor.matmul_mx(out=dp[h][:, n, :], lhsT=wb_w[:, ns].bitcast(E4M3), lhsT_scale=wb_s[:, ns],
                                    rhs=dh_w[h][:].bitcast(E4M3), rhs_scale=dh_s[h][:], start=True, stop=True)

        def larger(h):
            nc.vector.tensor_tensor(m0[h][:], dp[h][:], p_sb[:, :, h * H : (h + 1) * H], ALU.max)

        def put(h, n, on_scalar):
            window = pages[n][:].indirect(l5[:, h * H // 16 : (h + 1) * H // 16])
            if on_scalar:
                nc.scalar.activation(out=window, in_=m0[h][:, n, :], func=COPY)
            else:
                nc.vector.tensor_copy(window, m0[h][:, n, :])

        finish_products(0)
        add(0)
        finish_products(1)
        second(0)
        add(1)
        larger(0)
        second(1)
        put(0, 0, True)
        put(0, 1, True)
        larger(1)
        put(1, 0, True)
        put(1, 1, False)
        for n in range(NT):
            nc.sync.dma_start(out[n * P : (n + 1) * P, :], pages[n][:])
